import numpy as np, ml_dtypes
CORES = [40,64,80,88,96,104,120,144]
N = 8
import mx_ref
KO = 2
F = np.float32(0.7)
OWN = [1,1,1,1,1,1,1,1]
BF = ml_dtypes.bfloat16
def tile(rs):
    return np.stack(rs, axis=2).reshape(128, -1).astype(BF)
def pick(b):
    s = np.zeros((128, 128, 4), np.float32)
    s[np.arange(128), np.arange(128), b] = 1.0
    return mx_ref.quantize(s.reshape(128, 512).astype(BF))
def pk(c, s, i=0):
    return (np.ascontiguousarray(c[:, 512 * i:512 * i + 512]), mx_ref.live(s[:, 128 * i:128 * i + 128]))
def inputs(rng, e, E):
    def f(*shape):
        v = (rng.standard_normal(shape, dtype=np.float32) * np.exp2(rng.integers(-2, 3, shape[:-1] + (1,)))).astype(BF)
        return mx_ref.spread((v.astype(np.float32) * np.exp2(rng.integers(-E, E + 1, shape[:-2] + (1, 1))).astype(np.float32)).astype(BF), rng, e)
    def packed(k):
        c = np.zeros((N, 128, k * 512), np.uint8); s = np.zeros((N, 128, k * 128), np.uint8)
        for r in range(N):
            for i in range(k):
                a, b = mx_ref.quantize(f(128, 512)); c[r][:, 512 * i:512 * i + 512] = a; s[r][:, 128 * i:128 * i + 128] = mx_ref.plane(b, rng)
        return c, s
    d = {}
    d["kc"], d["ks"] = packed(KO)
    d["q"] = f(N, 128, 512)
    return d
def setup_inputs(rng):
    return inputs(rng, 0, 0)
def setup_inputs_blocks(rng):
    return inputs(rng, 4, 0)
def setup_inputs_wide(rng):
    return inputs(rng, 0, 8)
def reference(kc, ks, q):
    S = [pick(t) for t in range(4)]
    anew = lambda p, i: mx_ref.quantize(tile([mx_ref.matmul(S[t], pk(kc[p], ks[p], i)) * F for t in range(4)]))
    y = np.full((N, 128, 2048), np.nan, np.float32)
    for o in range(N):
        if OWN[o] != o: continue
        qq = mx_ref.quantize(q[o])
        M = [pk(kc[o], ks[o], i) for i in range(KO)] + [anew(p, i) for p in range(N) if p != o and OWN[p] == o for i in range(KO)]
        y[o][:, :128 * len(M)] = np.concatenate([mx_ref.matmul(qq, m) for m in M], axis=1)
    return {"y": y}

@@ -1,0 +1,185 @@
+import numpy as np
+from concourse.mybir import dt, AluOpType, ActivationFunctionType
+
+W = 256
+H = 128
+
+SCRATCH = {
+    "kin": ("sbuf", [128, W], "float8_e4m3fn_x4"),
+    "kpl": ("sbuf", [128, W], "uint8"),
+    "w": ("sbuf", [128, 516], "bfloat16"),
+    "sq": ("sbuf", [128, 4 * H], "float8_e4m3fn_x4"),
+    "sp": ("sbuf", [128, 4 * H], "uint8"),
+    "t": ("sbuf", [128, 4 * W], "bfloat16"),
+    "nq": ("sbuf", [128, W], "float8_e4m3fn_x4"),
+    "np": ("sbuf", [128, W], "uint8"),
+    "rc": ("sbuf", [128, W], "float8_e4m3fn_x4"),
+    "rp": ("sbuf", [128, W], "uint8"),
+    "mc": ("sbuf", [128, 8 * W], "float8_e4m3fn_x4"),
+    "mp": ("sbuf", [128, 8 * W], "uint8"),
+    "qt": ("sbuf", [128, 4 * H], "bfloat16"),
+    "qq": ("sbuf", [128, H], "float8_e4m3fn_x4"),
+    "qp": ("sbuf", [128, H], "uint8"),
+    "ys": ("sbuf", [128, 8 * W], "float32"),
+    "ps": ("psum", [128, 8 * 512], "float32"),
+}
+SEMAPHORES = (["ldc", "ldp", "wz", "wr", "wo", "sd", "sc0", "sc1", "qd", "ls", "rca", "rpa", "ldq", "qqd", "st"]
+              + ["mm%d" % k for k in range(12)] + ["arr%d" % r for r in range(8)] + ["cp%d" % r for r in range(8)])
+
+C07 = float(np.float32(0.7))
+
+
+def plan(T, topo):
+    own = T.tables["OWN"]
+    o = [r for r in range(len(own)) if own[r] == r][0]
+    cons = T.cores[o]
+    prod = [r for r in range(len(own)) if r != o and own[r] == o]
+    col = {o: 0}
+    for k, r in enumerate(prod):
+        col[r] = W * (k + 1)
+
+    def chip_of(c):
+        return [topo.host(c), topo.chip(c)]
+
+    every = range(len(T.cores) and 256)
+    far = [c for c in every if topo.mates(c, cons) and topo.may_write(c, cons)]
+    stop, used = {}, []
+    for r in prod:
+        c = T.cores[r]
+        if topo.may_write(c, cons):
+            stop[r] = None
+            continue
+        busy = [x for x in T.cores if topo.mates(x, c)]
+        near = [x for x in every if chip_of(x) == chip_of(c) and topo.may_write(x, cons) and topo.die(x) != topo.die(c)]
+        fars = [x for x in far if topo.may_write(c, x) and topo.die(x) not in [topo.die(u) for u in used]]
+        if busy and fars:
+            stop[r] = fars[0]
+            used.append(fars[0])
+        else:
+            stop[r] = near[0]
+    order = [r for r in prod if stop[r] is None] + [r for r in prod if stop[r] is not None]
+    return o, cons, col, stop, order
+
+
+def engines(m):
+    return bin(m).count("1")
+
+
+def send(g, topo, src, dst, out_ap, in_ap, rsem, lsem):
+    rid, pid = topo.addr(dst, src)
+    m = topo.mask(src, dst)
+    g.remote_dma(out_ap=out_ap, in_ap=in_ap, remote_sem=rsem, local_sem=lsem, pid=pid, routing_id=rid, dma_engine_mask=m)
+    return engines(m)
+
+
+def producer(g, core, T, topo, r, cons, col, stop):
+    s = T.sem
+    g.sync.dma_start(T.kin[:].bitcast(dt.uint8), T.kc[:]).then_inc(s.ldc, 16)
+    g.scalar.dma_start(T.kpl[:], T.ks[:]).then_inc(s.ldp, 16)
+    g.vector.memset(T.w[:, 3:516:4], 0.0).then_inc(s.wz, 1)
+    for b in range(3):
+        g.vector.memset(T.w[:, b:516:4], 0.0).then_inc(s.wr, 1)
+    g.wait_ge(s.wz, 1)
+    g.affine_select(T.w[:, 3:512:4], T.w[:, 3:512:4], [[-1, H]], AluOpType.not_equal, 1.0, 0, 1).then_inc(s.wo, 1)
+    g.vector.wait_ge(s.wr, 3)
+    g.vector.wait_ge(s.wo, 1)
+    for b in range(4):
+        g.vector.quantize_mx(T.sq[:, H * b:H * b + H], T.sp[:, H * b:H * b + H], T.w[:, 3 - b:3 - b + 4 * H]).then_inc(s.sd, 1)
+    g.tensor.wait_ge(s.sd, 4)
+    g.tensor.wait_ge(s.ldp, 16)
+    g.tensor.wait_ge(s.ldc, 16)
+    for i in range(2):
+        for b in range(4):
+            k = 4 * i + b
+            g.tensor.matmul_mx(T.ps[:, 512 * k:512 * k + H], T.sq[:, H * b:H * b + H], T.sp[:, H * b:H * b + H],
+                               T.kin[:, H * i:H * i + H], T.kpl[:, H * i:H * i + H], True, True).then_inc(s["mm%d" % k], 1)
+    for i in range(2):
+        sc = s["sc%d" % i]
+        for b in range(4):
+            k = 4 * i + b
+            src = T.ps[:, 512 * k:512 * k + H]
+            out = T.t[:, 512 * i + b:512 * i + 512:4]
+            if b % 2 == 0:
+                g.scalar.wait_ge(s["mm%d" % k], 1)
+                g.scalar.activation(out, src, ActivationFunctionType.Copy, scale=C07).then_inc(sc, 1)
+            else:
+                g.vector.wait_ge(s["mm%d" % k], 1)
+                g.vector.tensor_scalar(out, src, C07, None, AluOpType.mult).then_inc(sc, 1)
+        g.vector.wait_ge(sc, 4)
+        g.vector.quantize_mx(T.nq[:, H * i:H * i + H], T.np[:, H * i:H * i + H], T.t[:, 512 * i:512 * i + 512]).then_inc(s.qd, 1)
+    g.wait_ge(s.qd, 2)
+    a, n = col[r], 0
+    if stop[r] is None:
+        n += send(g, topo, core, cons, T.mp[:, a:a + W], T.np[:], s["arr%d" % r], s.ls)
+        n += send(g, topo, core, cons, T.mc[:, a:a + W].bitcast(dt.uint8), T.nq[:].bitcast(dt.uint8), s["arr%d" % r], s.ls)
+    else:
+        n += send(g, topo, core, stop[r], T.rp[:], T.np[:], s.rpa, s.ls)
+        n += send(g, topo, core, stop[r], T.rc[:].bitcast(dt.uint8), T.nq[:].bitcast(dt.uint8), s.rca, s.ls)
+    g.wait_ge(s.ls, n)
+
+
+def relay(g, core, T, topo, r, cons, col):
+    s = T.sem
+    m = engines(topo.mask(T.cores[r], core))
+    a, n = col[r], 0
+    g.wait_ge(s.rpa, m)
+    n += send(g, topo, core, cons, T.mp[:, a:a + W], T.rp[:], s["arr%d" % r], s.ls)
+    g.wait_ge(s.rca, m)
+    n += send(g, topo, core, cons, T.mc[:, a:a + W].bitcast(dt.uint8), T.rc[:].bitcast(dt.uint8), s["arr%d" % r], s.ls)
+    g.wait_ge(s.ls, n)
+
+
+def consumer(g, core, T, topo, o, col, stop, order):
+    s = T.sem
+    g.sync.dma_start(T.qt[:], T.q[:]).then_inc(s.ldq, 16)
+    g.scalar.dma_start(T.mc[:, 0:W].bitcast(dt.uint8), T.kc[:]).then_inc(s.ldc, 16)
+    g.sync.dma_start(T.mp[:, 0:W], T.ks[:]).then_inc(s.ldp, 16)
+    g.vector.wait_ge(s.ldq, 16)
+    g.vector.quantize_mx(T.qq[:], T.qp[:], T.qt[:]).then_inc(s.qqd, 1)
+    g.tensor.wait_ge(s.qqd, 1)
+    jobs = [o] + order
+    last = len(jobs) - 4
+    k, bank = 0, 0
+    owner = {}
+    for j, r in enumerate(jobs):
+        if r == o:
+            g.tensor.wait_ge(s.ldc, 16)
+            g.tensor.wait_ge(s.ldp, 16)
+        else:
+            m = engines(topo.mask(T.cores[r] if stop[r] is None else stop[r], core))
+            g.tensor.wait_ge(s["arr%d" % r], 2 * m)
+        parts = [(0, W)] if j < last else [(0, H), (H, H)]
+        for i, (d, n) in enumerate(parts):
+            a = col[r] + d
+            b = bank % 8
+            bank += 1
+            if b in owner:
+                g.tensor.wait_ge(s["cp%d" % owner[b][0]], owner[b][1])
+            owner[b] = (r, len(parts))
+            mm = s["mm%d" % k]
+            k += 1
+            out = T.ps[:, 512 * b:512 * b + n]
+            g.tensor.matmul_mx(out, T.qq[:], T.qp[:], T.mc[:, a:a + n], T.mp[:, a:a + n], True, True).then_inc(mm, 1)
+            if (i if len(parts) == 2 else j) % 2 == 0:
+                g.vector.wait_ge(mm, 1)
+                g.vector.tensor_copy(T.ys[:, a:a + n], out).then_inc(s["cp%d" % r], 1)
+            else:
+                g.scalar.wait_ge(mm, 1)
+                g.scalar.activation(T.ys[:, a:a + n], out, ActivationFunctionType.Copy).then_inc(s["cp%d" % r], 1)
+        a = col[r]
+        g.sync.wait_ge(s["cp%d" % r], len(parts))
+        g.sync.dma_start(T.y[:, a:a + W], T.ys[:, a:a + W]).then_inc(s.st, 16)
+    g.sync.wait_ge(s.st, 16 * len(jobs))
+
+
+def rank_program(g, core, T, topo):
+    o, cons, col, stop, order = plan(T, topo)
+    rank = T.rank_of(core)
+    if rank == o:
+        consumer(g, core, T, topo, o, col, stop, order)
+    elif rank is not None:
+        producer(g, core, T, topo, rank, cons, col, stop)
+    else:
+        for r in order:
+            if stop[r] == core:
+                relay(g, core, T, topo, r, cons, col)

@@ -13,8 +13,6 @@ SCRATCH = {
     "t": ("sbuf", [128, 4 * W], "bfloat16"),
     "nq": ("sbuf", [128, W], "float8_e4m3fn_x4"),
     "np": ("sbuf", [128, W], "uint8"),
-    "rc": ("sbuf", [128, W], "float8_e4m3fn_x4"),
-    "rp": ("sbuf", [128, W], "uint8"),
     "mc": ("sbuf", [128, 8 * W], "float8_e4m3fn_x4"),
     "mp": ("sbuf", [128, 8 * W], "uint8"),
     "qt": ("sbuf", [128, 4 * H], "bfloat16"),
@@ -23,10 +21,16 @@ SCRATCH = {
     "ys": ("sbuf", [128, 8 * W], "float32"),
     "ps": ("psum", [128, 8 * 512], "float32"),
 }
-SEMAPHORES = (["ldc", "ldp", "wz", "wr", "wo", "sd", "sc0", "sc1", "qd", "ls", "rca", "rpa", "ldq", "qqd", "st"]
-              + ["mm%d" % k for k in range(12)] + ["arr%d" % r for r in range(8)] + ["cp%d" % r for r in range(8)])
+SEMAPHORES = (["ldc0", "ldc1", "ldp", "wz", "wr", "wo", "sd", "sc0", "sc1", "qd0", "qd1", "ls", "ldq", "qqd", "st"]
+              + ["mm%d" % k for k in range(16)] + ["cp%d" % k for k in range(16)]
+              + ["early%d" % r for r in range(8)] + ["late%d" % r for r in range(8)] + ["rv%d" % k for k in range(3)])
 
 C07 = float(np.float32(0.7))
+PIECES = [(1, 0, H), (0, 0, W), (1, H, W)]
+
+
+def engines(m):
+    return bin(m).count("1")
 
 
 def plan(T, topo):
@@ -37,45 +41,49 @@ def plan(T, topo):
     col = {o: 0}
     for k, r in enumerate(prod):
         col[r] = W * (k + 1)
+    every = range(256)
 
-    def chip_of(c):
-        return [topo.host(c), topo.chip(c)]
+    def ports(near, d):
+        return [x for x in every if (topo.host(x), topo.chip(x)) == (topo.host(near), topo.chip(near)) and topo.may_write(x, cons) and topo.die(x) == d]
 
-    every = range(len(T.cores) and 256)
-    far = [c for c in every if topo.mates(c, cons) and topo.may_write(c, cons)]
-    stop, used = {}, []
+    beside = [c for c in every if topo.mates(c, cons)][0]
+    stop, used = {}, 0
     for r in prod:
         c = T.cores[r]
+        d = topo.die(c)
         if topo.may_write(c, cons):
             stop[r] = None
-            continue
-        busy = [x for x in T.cores if topo.mates(x, c)]
-        near = [x for x in every if chip_of(x) == chip_of(c) and topo.may_write(x, cons) and topo.die(x) != topo.die(c)]
-        fars = [x for x in far if topo.may_write(c, x) and topo.die(x) not in [topo.die(u) for u in used]]
-        if busy and fars:
-            stop[r] = fars[0]
-            used.append(fars[0])
+        elif [y for y in T.cores if topo.mates(y, c)]:
+            stop[r] = ports(beside, d if used == 0 else 1 - d)[0]
+            used += 1
         else:
-            stop[r] = near[0]
+            stop[r] = ports(c, 1 - d)[0]
     order = [r for r in prod if stop[r] is None] + [r for r in prod if stop[r] is not None]
     return o, cons, col, stop, order
 
 
-def engines(m):
-    return bin(m).count("1")
-
-
-def send(g, topo, src, dst, out_ap, in_ap, rsem, lsem):
+def send(g, topo, src, dst, piece, dst_buf, d, src_buf, rsem, lsem):
+    codes, a, e = piece
     rid, pid = topo.addr(dst, src)
     m = topo.mask(src, dst)
+    out_ap, in_ap = dst_buf[:, d + a:d + e], src_buf[:, a:e]
+    if codes:
+        out_ap, in_ap = out_ap.bitcast(dt.uint8), in_ap.bitcast(dt.uint8)
     g.remote_dma(out_ap=out_ap, in_ap=in_ap, remote_sem=rsem, local_sem=lsem, pid=pid, routing_id=rid, dma_engine_mask=m)
     return engines(m)
 
 
+def deliver(g, core, T, topo, r, k, cons, col):
+    codes = PIECES[k][0]
+    return send(g, topo, core, cons, PIECES[k], T.mc if codes else T.mp, col[r], T.nq if codes else T.np,
+                T.sem["late%d" % r] if k == 2 else T.sem["early%d" % r], T.sem.ls)
+
+
 def producer(g, core, T, topo, r, cons, col, stop):
     s = T.sem
-    g.sync.dma_start(T.kin[:].bitcast(dt.uint8), T.kc[:]).then_inc(s.ldc, 16)
+    g.sync.dma_start(T.kin[:, 0:H].bitcast(dt.uint8), T.kc[:, 0:4 * H]).then_inc(s.ldc0, 16)
     g.scalar.dma_start(T.kpl[:], T.ks[:]).then_inc(s.ldp, 16)
+    g.sync.dma_start(T.kin[:, H:W].bitcast(dt.uint8), T.kc[:, 4 * H:4 * W]).then_inc(s.ldc1, 16)
     g.vector.memset(T.w[:, 3:516:4], 0.0).then_inc(s.wz, 1)
     for b in range(3):
         g.vector.memset(T.w[:, b:516:4], 0.0).then_inc(s.wr, 1)
@@ -87,8 +95,8 @@ def producer(g, core, T, topo, r, cons, col, stop):
         g.vector.quantize_mx(T.sq[:, H * b:H * b + H], T.sp[:, H * b:H * b + H], T.w[:, 3 - b:3 - b + 4 * H]).then_inc(s.sd, 1)
     g.tensor.wait_ge(s.sd, 4)
     g.tensor.wait_ge(s.ldp, 16)
-    g.tensor.wait_ge(s.ldc, 16)
     for i in range(2):
+        g.tensor.wait_ge(s["ldc%d" % i], 16)
         for b in range(4):
             k = 4 * i + b
             g.tensor.matmul_mx(T.ps[:, 512 * k:512 * k + H], T.sq[:, H * b:H * b + H], T.sp[:, H * b:H * b + H],
@@ -106,69 +114,60 @@ def producer(g, core, T, topo, r, cons, col, stop):
                 g.vector.wait_ge(s["mm%d" % k], 1)
                 g.vector.tensor_scalar(out, src, C07, None, AluOpType.mult).then_inc(sc, 1)
         g.vector.wait_ge(sc, 4)
-        g.vector.quantize_mx(T.nq[:, H * i:H * i + H], T.np[:, H * i:H * i + H], T.t[:, 512 * i:512 * i + 512]).then_inc(s.qd, 1)
-    g.wait_ge(s.qd, 2)
-    a, n = col[r], 0
-    if stop[r] is None:
-        n += send(g, topo, core, cons, T.mp[:, a:a + W], T.np[:], s["arr%d" % r], s.ls)
-        n += send(g, topo, core, cons, T.mc[:, a:a + W].bitcast(dt.uint8), T.nq[:].bitcast(dt.uint8), s["arr%d" % r], s.ls)
-    else:
-        n += send(g, topo, core, stop[r], T.rp[:], T.np[:], s.rpa, s.ls)
-        n += send(g, topo, core, stop[r], T.rc[:].bitcast(dt.uint8), T.nq[:].bitcast(dt.uint8), s.rca, s.ls)
+        g.vector.quantize_mx(T.nq[:, H * i:H * i + H], T.np[:, H * i:H * i + H], T.t[:, 512 * i:512 * i + 512]).then_inc(s["qd%d" % i], 1)
+    n = 0
+    for k, piece in enumerate(PIECES):
+        if k < 2:
+            g.wait_ge(s["qd%d" % k], 1)
+        if stop[r] is None:
+            n += deliver(g, core, T, topo, r, k, cons, col)
+        else:
+            buf = T.nq if piece[0] else T.np
+            n += send(g, topo, core, stop[r], piece, buf, 0, buf, s["rv%d" % k], s.ls)
     g.wait_ge(s.ls, n)
 
 
 def relay(g, core, T, topo, r, cons, col):
-    s = T.sem
-    m = engines(topo.mask(T.cores[r], core))
-    a, n = col[r], 0
-    g.wait_ge(s.rpa, m)
-    n += send(g, topo, core, cons, T.mp[:, a:a + W], T.rp[:], s["arr%d" % r], s.ls)
-    g.wait_ge(s.rca, m)
-    n += send(g, topo, core, cons, T.mc[:, a:a + W].bitcast(dt.uint8), T.rc[:].bitcast(dt.uint8), s["arr%d" % r], s.ls)
-    g.wait_ge(s.ls, n)
+    n = 0
+    for k in range(len(PIECES)):
+        g.wait_ge(T.sem["rv%d" % k], engines(topo.mask(T.cores[r], core)))
+        n += deliver(g, core, T, topo, r, k, cons, col)
+    g.wait_ge(T.sem.ls, n)
 
 
 def consumer(g, core, T, topo, o, col, stop, order):
     s = T.sem
     g.sync.dma_start(T.qt[:], T.q[:]).then_inc(s.ldq, 16)
-    g.scalar.dma_start(T.mc[:, 0:W].bitcast(dt.uint8), T.kc[:]).then_inc(s.ldc, 16)
+    g.scalar.dma_start(T.mc[:, 0:W].bitcast(dt.uint8), T.kc[:]).then_inc(s.ldc0, 16)
     g.sync.dma_start(T.mp[:, 0:W], T.ks[:]).then_inc(s.ldp, 16)
     g.vector.wait_ge(s.ldq, 16)
     g.vector.quantize_mx(T.qq[:], T.qp[:], T.qt[:]).then_inc(s.qqd, 1)
     g.tensor.wait_ge(s.qqd, 1)
-    jobs = [o] + order
-    last = len(jobs) - 4
-    k, bank = 0, 0
-    owner = {}
-    for j, r in enumerate(jobs):
+    jobs = [(o, 0, W)] + [(r, 0, H) for r in order] + [(r, H, W) for r in order]
+    for j, (r, a, e) in enumerate(jobs):
         if r == o:
-            g.tensor.wait_ge(s.ldc, 16)
+            g.tensor.wait_ge(s.ldc0, 16)
             g.tensor.wait_ge(s.ldp, 16)
         else:
             m = engines(topo.mask(T.cores[r] if stop[r] is None else stop[r], core))
-            g.tensor.wait_ge(s["arr%d" % r], 2 * m)
-        parts = [(0, W)] if j < last else [(0, H), (H, H)]
-        for i, (d, n) in enumerate(parts):
-            a = col[r] + d
-            b = bank % 8
-            bank += 1
-            if b in owner:
-                g.tensor.wait_ge(s["cp%d" % owner[b][0]], owner[b][1])
-            owner[b] = (r, len(parts))
-            mm = s["mm%d" % k]
-            k += 1
-            out = T.ps[:, 512 * b:512 * b + n]
-            g.tensor.matmul_mx(out, T.qq[:], T.qp[:], T.mc[:, a:a + n], T.mp[:, a:a + n], True, True).then_inc(mm, 1)
-            if (i if len(parts) == 2 else j) % 2 == 0:
-                g.vector.wait_ge(mm, 1)
-                g.vector.tensor_copy(T.ys[:, a:a + n], out).then_inc(s["cp%d" % r], 1)
+            if a == 0:
+                g.tensor.wait_ge(s["early%d" % r], 2 * m)
             else:
-                g.scalar.wait_ge(mm, 1)
-                g.scalar.activation(T.ys[:, a:a + n], out, ActivationFunctionType.Copy).then_inc(s["cp%d" % r], 1)
-        a = col[r]
-        g.sync.wait_ge(s["cp%d" % r], len(parts))
-        g.sync.dma_start(T.y[:, a:a + W], T.ys[:, a:a + W]).then_inc(s.st, 16)
+                g.tensor.wait_ge(s["late%d" % r], m)
+        if j >= 8:
+            g.tensor.wait_ge(s["cp%d" % (j - 8)], 1)
+        b, a, e = j % 8, col[r] + a, col[r] + e
+        out = T.ps[:, 512 * b:512 * b + e - a]
+        mm, cp = s["mm%d" % j], s["cp%d" % j]
+        g.tensor.matmul_mx(out, T.qq[:], T.qp[:], T.mc[:, a:e], T.mp[:, a:e], True, True).then_inc(mm, 1)
+        if j % 2 == 0:
+            g.vector.wait_ge(mm, 1)
+            g.vector.tensor_copy(T.ys[:, a:e], out).then_inc(cp, 1)
+        else:
+            g.scalar.wait_ge(mm, 1)
+            g.scalar.activation(T.ys[:, a:e], out, ActivationFunctionType.Copy).then_inc(cp, 1)
+        g.sync.wait_ge(cp, 1)
+        g.sync.dma_start(T.y[:, a:e], T.ys[:, a:e]).then_inc(s.st, 16)
     g.sync.wait_ge(s.st, 16 * len(jobs))
 
 

import numpy as np
from concourse.mybir import dt, AluOpType, ActivationFunctionType

W = 256
H = 128

SCRATCH = {
    "kin": ("sbuf", [128, W], "float8_e4m3fn_x4"),
    "kpl": ("sbuf", [128, W], "uint8"),
    "w": ("sbuf", [128, 516], "bfloat16"),
    "sq": ("sbuf", [128, 4 * H], "float8_e4m3fn_x4"),
    "sp": ("sbuf", [128, 4 * H], "uint8"),
    "t": ("sbuf", [128, 4 * W], "bfloat16"),
    "nq": ("sbuf", [128, W], "float8_e4m3fn_x4"),
    "np": ("sbuf", [128, W], "uint8"),
    "mc": ("sbuf", [128, 8 * W], "float8_e4m3fn_x4"),
    "mp": ("sbuf", [128, 8 * W], "uint8"),
    "qt": ("sbuf", [128, 4 * H], "bfloat16"),
    "qq": ("sbuf", [128, H], "float8_e4m3fn_x4"),
    "qp": ("sbuf", [128, H], "uint8"),
    "ys": ("sbuf", [128, 8 * W], "float32"),
    "ps": ("psum", [128, 8 * 512], "float32"),
}
SEMAPHORES = (["ldc0", "ldc1", "ldp", "wz", "wr", "wo", "sd", "sc0", "sc1", "qd0", "qd1", "ls", "ldq", "qqd", "st"]
              + ["mm%d" % k for k in range(16)] + ["cp%d" % k for k in range(16)]
              + ["early%d" % r for r in range(8)] + ["late%d" % r for r in range(8)] + ["rv%d" % k for k in range(3)])

C07 = float(np.float32(0.7))
PIECES = [(1, 0, H), (0, 0, W), (1, H, W)]


def engines(m):
    return bin(m).count("1")


def plan(T, topo):
    own = T.tables["OWN"]
    o = [r for r in range(len(own)) if own[r] == r][0]
    cons = T.cores[o]
    prod = [r for r in range(len(own)) if r != o and own[r] == o]
    col = {o: 0}
    for k, r in enumerate(prod):
        col[r] = W * (k + 1)
    every = range(256)

    def ports(near, d):
        return [x for x in every if (topo.host(x), topo.chip(x)) == (topo.host(near), topo.chip(near)) and topo.may_write(x, cons) and topo.die(x) == d]

    beside = [c for c in every if topo.mates(c, cons)][0]
    stop, used = {}, 0
    for r in prod:
        c = T.cores[r]
        d = topo.die(c)
        if topo.may_write(c, cons):
            stop[r] = None
        elif [y for y in T.cores if topo.mates(y, c)]:
            stop[r] = ports(beside, d if used == 0 else 1 - d)[0]
            used += 1
        else:
            stop[r] = ports(c, 1 - d)[0]
    order = [r for r in prod if stop[r] is None] + [r for r in prod if stop[r] is not None]
    return o, cons, col, stop, order


def send(g, topo, src, dst, piece, dst_buf, d, src_buf, rsem, lsem):
    codes, a, e = piece
    rid, pid = topo.addr(dst, src)
    m = topo.mask(src, dst)
    out_ap, in_ap = dst_buf[:, d + a:d + e], src_buf[:, a:e]
    if codes:
        out_ap, in_ap = out_ap.bitcast(dt.uint8), in_ap.bitcast(dt.uint8)
    g.remote_dma(out_ap=out_ap, in_ap=in_ap, remote_sem=rsem, local_sem=lsem, pid=pid, routing_id=rid, dma_engine_mask=m)
    return engines(m)


def deliver(g, core, T, topo, r, k, cons, col):
    codes = PIECES[k][0]
    return send(g, topo, core, cons, PIECES[k], T.mc if codes else T.mp, col[r], T.nq if codes else T.np,
                T.sem["late%d" % r] if k == 2 else T.sem["early%d" % r], T.sem.ls)


def producer(g, core, T, topo, r, cons, col, stop):
    s = T.sem
    g.sync.dma_start(T.kin[:, 0:H].bitcast(dt.uint8), T.kc[:, 0:4 * H]).then_inc(s.ldc0, 16)
    g.scalar.dma_start(T.kpl[:], T.ks[:]).then_inc(s.ldp, 16)
    g.sync.dma_start(T.kin[:, H:W].bitcast(dt.uint8), T.kc[:, 4 * H:4 * W]).then_inc(s.ldc1, 16)
    g.vector.memset(T.w[:, 3:516:4], 0.0).then_inc(s.wz, 1)
    for b in range(3):
        g.vector.memset(T.w[:, b:516:4], 0.0).then_inc(s.wr, 1)
    g.wait_ge(s.wz, 1)
    g.affine_select(T.w[:, 3:512:4], T.w[:, 3:512:4], [[-1, H]], AluOpType.not_equal, 1.0, 0, 1).then_inc(s.wo, 1)
    g.vector.wait_ge(s.wr, 3)
    g.vector.wait_ge(s.wo, 1)
    for b in range(4):
        g.vector.quantize_mx(T.sq[:, H * b:H * b + H], T.sp[:, H * b:H * b + H], T.w[:, 3 - b:3 - b + 4 * H]).then_inc(s.sd, 1)
    g.tensor.wait_ge(s.sd, 4)
    g.tensor.wait_ge(s.ldp, 16)
    for i in range(2):
        g.tensor.wait_ge(s["ldc%d" % i], 16)
        for b in range(4):
            k = 4 * i + b
            g.tensor.matmul_mx(T.ps[:, 512 * k:512 * k + H], T.sq[:, H * b:H * b + H], T.sp[:, H * b:H * b + H],
                               T.kin[:, H * i:H * i + H], T.kpl[:, H * i:H * i + H], True, True).then_inc(s["mm%d" % k], 1)
    for i in range(2):
        sc = s["sc%d" % i]
        for b in range(4):
            k = 4 * i + b
            src = T.ps[:, 512 * k:512 * k + H]
            out = T.t[:, 512 * i + b:512 * i + 512:4]
            if b % 2 == 0:
                g.scalar.wait_ge(s["mm%d" % k], 1)
                g.scalar.activation(out, src, ActivationFunctionType.Copy, scale=C07).then_inc(sc, 1)
            else:
                g.vector.wait_ge(s["mm%d" % k], 1)
                g.vector.tensor_scalar(out, src, C07, None, AluOpType.mult).then_inc(sc, 1)
        g.vector.wait_ge(sc, 4)
        g.vector.quantize_mx(T.nq[:, H * i:H * i + H], T.np[:, H * i:H * i + H], T.t[:, 512 * i:512 * i + 512]).then_inc(s["qd%d" % i], 1)
    n = 0
    for k, piece in enumerate(PIECES):
        if k < 2:
            g.wait_ge(s["qd%d" % k], 1)
        if stop[r] is None:
            n += deliver(g, core, T, topo, r, k, cons, col)
        else:
            buf = T.nq if piece[0] else T.np
            n += send(g, topo, core, stop[r], piece, buf, 0, buf, s["rv%d" % k], s.ls)
    g.wait_ge(s.ls, n)


def relay(g, core, T, topo, r, cons, col):
    n = 0
    for k in range(len(PIECES)):
        g.wait_ge(T.sem["rv%d" % k], engines(topo.mask(T.cores[r], core)))
        n += deliver(g, core, T, topo, r, k, cons, col)
    g.wait_ge(T.sem.ls, n)


def consumer(g, core, T, topo, o, col, stop, order):
    s = T.sem
    g.sync.dma_start(T.qt[:], T.q[:]).then_inc(s.ldq, 16)
    g.scalar.dma_start(T.mc[:, 0:W].bitcast(dt.uint8), T.kc[:]).then_inc(s.ldc0, 16)
    g.sync.dma_start(T.mp[:, 0:W], T.ks[:]).then_inc(s.ldp, 16)
    g.vector.wait_ge(s.ldq, 16)
    g.vector.quantize_mx(T.qq[:], T.qp[:], T.qt[:]).then_inc(s.qqd, 1)
    g.tensor.wait_ge(s.qqd, 1)
    jobs = [(o, 0, W)] + [(r, 0, H) for r in order] + [(r, H, W) for r in order]
    for j, (r, a, e) in enumerate(jobs):
        if r == o:
            g.tensor.wait_ge(s.ldc0, 16)
            g.tensor.wait_ge(s.ldp, 16)
        else:
            m = engines(topo.mask(T.cores[r] if stop[r] is None else stop[r], core))
            if a == 0:
                g.tensor.wait_ge(s["early%d" % r], 2 * m)
            else:
                g.tensor.wait_ge(s["late%d" % r], m)
        if j >= 8:
            g.tensor.wait_ge(s["cp%d" % (j - 8)], 1)
        b, a, e = j % 8, col[r] + a, col[r] + e
        out = T.ps[:, 512 * b:512 * b + e - a]
        mm, cp = s["mm%d" % j], s["cp%d" % j]
        g.tensor.matmul_mx(out, T.qq[:], T.qp[:], T.mc[:, a:e], T.mp[:, a:e], True, True).then_inc(mm, 1)
        if j % 2 == 0:
            g.vector.wait_ge(mm, 1)
            g.vector.tensor_copy(T.ys[:, a:e], out).then_inc(cp, 1)
        else:
            g.scalar.wait_ge(mm, 1)
            g.scalar.activation(T.ys[:, a:e], out, ActivationFunctionType.Copy).then_inc(cp, 1)
        g.sync.wait_ge(cp, 1)
        g.sync.dma_start(T.y[:, a:e], T.ys[:, a:e]).then_inc(s.st, 16)
    g.sync.wait_ge(s.st, 16 * len(jobs))


def rank_program(g, core, T, topo):
    o, cons, col, stop, order = plan(T, topo)
    rank = T.rank_of(core)
    if rank == o:
        consumer(g, core, T, topo, o, col, stop, order)
    elif rank is not None:
        producer(g, core, T, topo, rank, cons, col, stop)
    else:
        for r in order:
            if stop[r] == core:
                relay(g, core, T, topo, r, cons, col)
